import numpy as np
import ml_dtypes


def mxq(x, axis, fmt="e4m3"):
    dtype, down = {"e4m3": (ml_dtypes.float8_e4m3fn, 7), "e5m2": (ml_dtypes.float8_e5m2, 14)}[fmt]
    v = np.moveaxis(np.asarray(x, np.float32).astype(ml_dtypes.bfloat16).astype(np.float64), axis, -1)
    blocks = v.reshape(v.shape[:-1] + (-1, 32))
    amax = np.abs(blocks).max(-1, keepdims=True)
    byte = np.maximum(np.where(amax > 0, np.frexp(amax)[1] - 1 + 127, 0) - down, 1)
    scale = np.exp2(byte - 127.0)
    codes = (blocks / scale).astype(np.float32).astype(dtype).astype(np.float64)
    return np.moveaxis((codes * scale).reshape(v.shape), -1, axis)


WIDE = False


def mx_kscale(k):
    if not WIDE:
        return np.ones(k)
    levels = np.array([30, -30])
    if k % 512:
        return np.exp2(np.random.permutation(np.resize(levels, k // 32))).repeat(32)
    a = np.empty((k // 512, 16))
    for p in range(k // 512):
        a[p, :8] = np.random.permutation(np.resize(levels, 8))
        for g in range(8):
            far = levels[np.abs(levels - a[p, g]) >= 10]
            a[p, g + 8] = far[np.random.randint(len(far))]
    return np.exp2(a.ravel()).repeat(32)


def f64(x):
    return np.asarray(x).astype(np.float64)


def striped(idx):
    return np.tile(np.asarray(idx).reshape(-1, 16).T, (8, 1)).astype(np.uint16)


def unstriped(offs):
    return offs[:16].T.reshape(-1).astype(np.int64)


E2M1 = np.array([0.0, 0.5, 1.0, 1.5, 2.0, 3.0, 4.0, 6.0, -0.0, -0.5, -1.0, -1.5, -2.0, -3.0, -4.0, -6.0])


def pack_weight(w, fmt):
    k, n = w.shape
    w = f64(np.asarray(w, np.float32).astype(ml_dtypes.bfloat16)).reshape(k // 32, 32, n)
    amax = np.abs(w).max(1)
    if fmt in ("e4m3", "e5m2"):
        byte = np.frexp(amax)[1] - 1 + 127 - (7 if fmt == "e4m3" else 14)
    else:
        mant, ex = np.frexp(amax / 6.0)
        byte = np.where(mant > 0.5, ex, ex - 1) + 127
    byte = np.clip(np.where(amax > 0, byte, 1), 1, 254)
    scaled = (w * np.exp2(127.0 - byte)[:, None, :]).reshape(k, n).astype(np.float32)
    by_word = np.ascontiguousarray(scaled.reshape(k // 512, 128, 4, n).transpose(0, 1, 3, 2))
    if fmt in ("e4m3", "e5m2"):
        words = by_word.astype(ml_dtypes.float8_e4m3fn if fmt == "e4m3" else ml_dtypes.float8_e5m2).view(np.uint8)
    else:
        c = by_word.astype(ml_dtypes.float4_e2m1fn).view(np.uint8) & 0xF
        words = (c[..., 0::2] | (c[..., 1::2] << 4)).reshape(k // 512, 128, 2 * n)
    return np.ascontiguousarray(words), np.ascontiguousarray(byte.astype(np.uint8).reshape(k // 512, 16, n))


def unpack_weight(words, scales, fmt):
    g, _, n = scales.shape
    words = np.ascontiguousarray(words).reshape(g, 128, n, -1)
    if fmt in ("e4m3", "e5m2"):
        vals = words.view(ml_dtypes.float8_e4m3fn if fmt == "e4m3" else ml_dtypes.float8_e5m2).astype(np.float64)
    else:
        nib = np.empty((g, 128, n, 4), np.uint8)
        nib[..., 0::2] = words & 0xF
        nib[..., 1::2] = words >> 4
        vals = E2M1[nib]
    vals = vals * np.repeat(np.exp2(scales.astype(np.float64) - 127.0), 8, axis=1)[..., None]
    return vals.transpose(0, 1, 3, 2).reshape(g * 512, n)


K, F, T, Z, J, R, V, O, N = 512, 512, 1024, 1024, 256, 512, 512, 128, 256


def setup_inputs():
    n = np.random.standard_normal
    idx = np.random.permutation(T)[:J]
    idx2 = np.random.permutation(Z)[:J]
    idx3 = np.random.permutation(J)[:O]
    idx4 = np.random.permutation(V)[:O]
    idx5 = np.random.permutation(J)[:O]
    idx6 = np.random.permutation(T)[:O]
    fk = mx_kscale(K)
    fr = mx_kscale(R)
    ff = mx_kscale(F)
    xtp = pack_weight(n((K, T)) / fk[:, None], "e2m1")
    wp = pack_weight(n((K, R)) * 1 / np.sqrt(K) * fk[:, None] * fr, "e5m2")
    xop = pack_weight(n((F, Z)) / ff[:, None], "e5m2")
    w2p = pack_weight(n((F, R)) * 1 / np.sqrt(F) * ff[:, None] * fr, "e4m3")
    wbp = pack_weight(n((R, N)) * 1 / np.sqrt(R) / fr[:, None], "e4m3")
    wsp = pack_weight(n((K, N)) * 1 / np.sqrt(K) * fk[:, None], "e4m3")
    return {
        "xt_words": xtp[0],
        "xt_scales": xtp[1],
        "w_words": wp[0],
        "w_scales": wp[1],
        "xo_words": xop[0],
        "xo_scales": xop[1],
        "w2_words": w2p[0],
        "w2_scales": w2p[1],
        "tb": (n((R, V)) * 0.8 * fr[:, None]).astype(np.float32),
        "wb_words": wbp[0],
        "wb_scales": wbp[1],
        "ws_words": wsp[0],
        "ws_scales": wsp[1],
        "offs": striped(idx),
        "offs2": striped(idx2),
        "offs3": striped(idx3),
        "offs4": striped(idx4),
        "offs5": striped(idx5),
        "offs6": striped(idx6),
    }


def reference(xt_words, xt_scales, w_words, w_scales, xo_words, xo_scales, w2_words, w2_scales, tb, wb_words, wb_scales, ws_words, ws_scales, offs, offs2, offs3, offs4, offs5, offs6):
    idx = unstriped(offs)
    idx2 = unstriped(offs2)
    idx3 = unstriped(offs3)
    idx4 = unstriped(offs4)
    idx5 = unstriped(offs5)
    idx6 = unstriped(offs6)
    xtu = unpack_weight(xt_words, xt_scales, "e2m1")
    wu = unpack_weight(w_words, w_scales, "e5m2")
    xou = unpack_weight(xo_words, xo_scales, "e5m2")
    w2u = unpack_weight(w2_words, w2_scales, "e4m3")
    wbu = unpack_weight(wb_words, wb_scales, "e4m3")
    wsu = unpack_weight(ws_words, ws_scales, "e4m3")
    xtidxg = xtu[:, idx]
    a = wu.T @ xtidxg
    xoidx2g = xou[:, idx2]
    b = w2u.T @ xoidx2g
    hid = np.maximum(np.minimum(a[:, idx3], f64(tb)[:, idx4]), b[:, idx5])
    hidq = mxq(hid, 0, "e5m2")
    xtidx6g = xtu[:, idx6]
    y = wbu.T @ hidq + wsu.T @ xtidx6g
    return y

@@ -1,0 +1,175 @@
+from contextlib import ExitStack
+
+import concourse.mybir as mybir
+
+F32 = mybir.dt.float32
+BF16 = mybir.dt.bfloat16
+I32 = mybir.dt.int32
+U32 = mybir.dt.uint32
+U16 = mybir.dt.uint16
+U8 = mybir.dt.uint8
+E4M3 = mybir.dt.float8_e4m3fn_x4
+E5M2 = mybir.dt.float8_e5m2_x4
+E2M1 = mybir.dt.float4_e2m1fn_x4
+COPY = mybir.ActivationFunctionType.Copy
+ALU = mybir.AluOpType
+
+P = 128
+PACK = 4
+T, Z, J, R, V, O, N = 1024, 1024, 256, 512, 512, 128, 256
+FLOPS = 2 * 512 * (R * J + R * J + N * O + N * O)
+
+
+def load_words(queue, tile, dram):
+    queue.dma_start(out=tile[:].bitcast(I32), in_=dram.bitcast(I32))
+
+
+def load_scales(queue, plane, dram):
+    for q in range(4):
+        queue.dma_start(out=plane[32 * q : 32 * q + 4, :].bitcast(I32), in_=dram[0, 4 * q : 4 * q + 4, :].bitcast(I32))
+
+
+def tile_list_capped_twotab_further_plain_kernel(
+    tc, xt_words, xt_scales, w_words, w_scales, xo_words, xo_scales, w2_words, w2_scales, tb,
+    wb_words, wb_scales, ws_words, ws_scales, offs, offs2, offs3, offs4, offs5, offs6, out,
+):
+    nc = tc.nc
+    with ExitStack() as ctx:
+        sb = ctx.enter_context(tc.tile_pool(name="sb", bufs=1))
+        ps = ctx.enter_context(tc.psum_pool(name="ps", bufs=1))
+
+        def tile(name, shape, dtype):
+            return sb.tile(shape, dtype, name=name, align_bytes=64)
+
+        def load_list(name, dram):
+            lst = tile(name, [P, dram.shape[1]], U16)
+            nc.sync.dma_start(lst[:], dram)
+            return lst
+
+        def merged(words):
+            return words[0].rearrange("p n t -> p (n t)")
+
+        xt_s = tile("xt_s", [P, T], U8)
+        w_s = tile("w_s", [P, R], U8)
+        xo_s = tile("xo_s", [P, Z], U8)
+        w2_s = tile("w2_s", [P, R], U8)
+        ws_s = tile("ws_s", [P, N], U8)
+        wb_s = tile("wb_s", [P, N], U8)
+        for plane in (xt_s, w_s, xo_s, w2_s, ws_s, wb_s):
+            nc.vector.memset(plane[:].bitcast(I32), 0)
+
+        xt_w = tile("xt_w", [P, T], U16)
+        w_w = tile("w_w", [P, R], U32)
+        xo_w = tile("xo_w", [P, Z], U32)
+        w2_w = tile("w2_w", [P, R], U32)
+        ws_w = tile("ws_w", [P, N], U32)
+        wb_w = tile("wb_w", [P, N], U32)
+        caps = tile("caps", [P, PACK * V], F32)
+
+        l1 = load_list("l1", offs)
+        load_words(nc.sync, xt_w, xt_words[0])
+        load_words(nc.sync, w_w, merged(w_words))
+        l2 = load_list("l2", offs2)
+        l6 = load_list("l6", offs6)
+        l3 = load_list("l3", offs3)
+        l4 = load_list("l4", offs4)
+        l5 = load_list("l5", offs5)
+        load_words(nc.gpsimd, xo_w, merged(xo_words))
+        load_words(nc.gpsimd, w2_w, merged(w2_words))
+        nc.gpsimd.dma_start(out=caps[:], in_=tb.rearrange("(p t) v -> p (t v)", t=PACK))
+        load_words(nc.gpsimd, ws_w, merged(ws_words))
+        load_words(nc.gpsimd, wb_w, merged(wb_words))
+        load_scales(nc.sync, xt_s, xt_scales)
+        load_scales(nc.sync, w_s, w_scales)
+        load_scales(nc.sync, xo_s, xo_scales)
+        load_scales(nc.sync, w2_s, w2_scales)
+        load_scales(nc.sync, ws_s, ws_scales)
+        load_scales(nc.sync, wb_s, wb_scales)
+
+        def gather(name, window, lst, width, dtype):
+            got = tile(name, [P, width], dtype)
+            nc.vector.tensor_copy(got[:], window[:].indirect(lst[:]))
+            return got
+
+        def deal(name, words, plane):
+            dw = tile(name + "_w", [P, PACK, P], U32)
+            ds = tile(name + "_s", [P, PACK, P], U8)
+            nc.scalar.copy(dw[:].rearrange("p t q -> p q t"), words[:].rearrange("p (q t) -> p q t", t=PACK))
+            nc.vector.tensor_copy(ds[:].rearrange("p t q -> p q t"), plane[:].rearrange("p (q t) -> p q t", t=PACK))
+            return dw, ds
+
+        xg_w = gather("xg_w", xt_w, l1, J, U16)
+        xg_s = gather("xg_s", xt_s, l1, J, U8)
+        wd_w, wd_s = deal("wd", w_w, w_s)
+        a_pick = tile("a_pick", [P, PACK, O], F32)
+        a_banks = [ps.tile([P, 2, J], F32, name="a_bank%d" % h) for h in range(2)]
+        for t in range(PACK):
+            nc.tensor.matmul_mx(
+                out=a_banks[t // 2][:, t % 2, :], lhsT=wd_w[:, t, :].bitcast(E5M2), lhsT_scale=wd_s[:, t, :],
+                rhs=xg_w[:].bitcast(E2M1), rhs_scale=xg_s[:], start=True, stop=True,
+            )
+        a_rows = [tile("a_rows%d" % t, [P, J], F32) for t in range(PACK)]
+        for t in range(PACK):
+            nc.scalar.activation(a_rows[t][:], a_banks[t // 2][:, t % 2, :], COPY)
+        for t in range(PACK):
+            nc.scalar.activation(a_pick[:, t, :], a_rows[t][:].indirect(l3[:]), COPY)
+
+        og_w = gather("og_w", xo_w, l2, J, U32)
+        og_s = gather("og_s", xo_s, l2, J, U8)
+        w2d_w, w2d_s = deal("w2d", w2_w, w2_s)
+        b_banks = [ps.tile([P, J], F32, name="b_bank%d" % t) for t in range(PACK)]
+        for t in range(PACK):
+            nc.tensor.matmul_mx(
+                out=b_banks[t][:], lhsT=w2d_w[:, t, :].bitcast(E4M3), lhsT_scale=w2d_s[:, t, :],
+                rhs=og_w[:].bitcast(E5M2), rhs_scale=og_s[:], start=True, stop=True,
+            )
+
+        sg_w = gather("sg_w", xt_w, l6, O, U16)
+        sg_s = gather("sg_s", xt_s, l6, O, U8)
+        y_banks = [ps.tile([P, O], F32, name="y_bank%d" % h) for h in range(2)]
+        for h in range(2):
+            cols = slice(h * P, (h + 1) * P)
+            nc.tensor.matmul_mx(
+                out=y_banks[h][:], lhsT=ws_w[:, cols].bitcast(E4M3), lhsT_scale=ws_s[:, cols],
+                rhs=sg_w[:].bitcast(E2M1), rhs_scale=sg_s[:], start=True, stop=False,
+            )
+        cap_pick = tile("cap_pick", [P, PACK, O], F32)
+        for t in range(PACK):
+            nc.vector.tensor_copy(cap_pick[:, t, :], caps[:, t * V : (t + 1) * V].indirect(l4[:]))
+        capped = tile("capped", [P, PACK, O], F32)
+        nc.vector.tensor_tensor(capped[:], a_pick[:], cap_pick[:], ALU.min)
+
+        b_rows = [tile("b_rows%d" % t, [P, J], F32) for t in range(PACK)]
+        b_pick = tile("b_pick", [P, PACK, O], F32)
+        for t in range(2):
+            nc.scalar.activation(b_rows[t][:], b_banks[t][:], COPY)
+        for t in range(2):
+            nc.scalar.activation(b_pick[:, t, :], b_rows[t][:].indirect(l5[:]), COPY)
+        for t in range(2, PACK):
+            nc.vector.tensor_copy(b_rows[t][:], b_banks[t][:])
+        for t in range(2, PACK):
+            nc.vector.tensor_copy(b_pick[:, t, :], b_rows[t][:].indirect(l5[:]))
+
+        hid = tile("hid", [P, O, PACK], BF16)
+        nc.vector.tensor_tensor(
+            hid[:].rearrange("p (c i) t -> p c t i", i=4),
+            capped[:].rearrange("p t (c i) -> p c t i", i=4),
+            b_pick[:].rearrange("p t (c i) -> p c t i", i=4),
+            ALU.max,
+        )
+        hid_w = tile("hid_w", [P, O], U32)
+        hid_s = tile("hid_s", [P, O], U8)
+        nc.vector.quantize_mx(out=hid_w[:].bitcast(E5M2), scales=hid_s[:], in_=hid[:].rearrange("p o t -> p (o t)"))
+
+        for h in range(2):
+            cols = slice(h * P, (h + 1) * P)
+            nc.tensor.matmul_mx(
+                out=y_banks[h][:], lhsT=wb_w[:, cols].bitcast(E4M3), lhsT_scale=wb_s[:, cols],
+                rhs=hid_w[:].bitcast(E5M2), rhs_scale=hid_s[:], start=False, stop=True,
+            )
+        y0 = tile("y0", [P, O], F32)
+        y1 = tile("y1", [P, O], F32)
+        nc.scalar.activation(y0[:], y_banks[0][:], COPY)
+        nc.scalar.dma_start(out=out[0:P, :], in_=y0[:])
+        nc.vector.tensor_copy(y1[:], y_banks[1][:])
+        nc.sync.dma_start(out=out[P : 2 * P, :], in_=y1[:])

@@ -66,25 +66,25 @@ def tile_list_capped_twotab_further_plain_kernel(
         wb_w = tile("wb_w", [P, N], U32)
         caps = tile("caps", [P, PACK * V], F32)
 
+        load_words(nc.sync, w_w, merged(w_words))
         l1 = load_list("l1", offs)
         load_words(nc.sync, xt_w, xt_words[0])
-        load_words(nc.sync, w_w, merged(w_words))
-        l2 = load_list("l2", offs2)
+        load_scales(nc.sync, xt_s, xt_scales)
         l6 = load_list("l6", offs6)
+        load_scales(nc.sync, w_s, w_scales)
+        l2 = load_list("l2", offs2)
+        load_scales(nc.sync, xo_s, xo_scales)
         l3 = load_list("l3", offs3)
-        l4 = load_list("l4", offs4)
+        load_scales(nc.sync, w2_s, w2_scales)
         l5 = load_list("l5", offs5)
+        l4 = load_list("l4", offs4)
+        load_scales(nc.sync, ws_s, ws_scales)
+        load_scales(nc.sync, wb_s, wb_scales)
         load_words(nc.gpsimd, xo_w, merged(xo_words))
         load_words(nc.gpsimd, w2_w, merged(w2_words))
         nc.gpsimd.dma_start(out=caps[:], in_=tb.rearrange("(p t) v -> p (t v)", t=PACK))
         load_words(nc.gpsimd, ws_w, merged(ws_words))
         load_words(nc.gpsimd, wb_w, merged(wb_words))
-        load_scales(nc.sync, xt_s, xt_scales)
-        load_scales(nc.sync, w_s, w_scales)
-        load_scales(nc.sync, xo_s, xo_scales)
-        load_scales(nc.sync, w2_s, w2_scales)
-        load_scales(nc.sync, ws_s, ws_scales)
-        load_scales(nc.sync, wb_s, wb_scales)
 
         def gather(name, window, lst, width, dtype):
             got = tile(name, [P, width], dtype)
@@ -109,8 +109,9 @@ def tile_list_capped_twotab_further_plain_kernel(
                 rhs=xg_w[:].bitcast(E2M1), rhs_scale=xg_s[:], start=True, stop=True,
             )
         a_rows = [tile("a_rows%d" % t, [P, J], F32) for t in range(PACK)]
-        for t in range(PACK):
-            nc.scalar.activation(a_rows[t][:], a_banks[t // 2][:, t % 2, :], COPY)
+        for t in range(2):
+            nc.scalar.activation(a_rows[t][:], a_banks[0][:, t, :], COPY)
+            nc.vector.tensor_copy(a_rows[2 + t][:], a_banks[1][:, t, :])
         for t in range(PACK):
             nc.scalar.activation(a_pick[:, t, :], a_rows[t][:].indirect(l3[:]), COPY)
 
@@ -133,11 +134,6 @@ def tile_list_capped_twotab_further_plain_kernel(
                 out=y_banks[h][:], lhsT=ws_w[:, cols].bitcast(E4M3), lhsT_scale=ws_s[:, cols],
                 rhs=sg_w[:].bitcast(E2M1), rhs_scale=sg_s[:], start=True, stop=False,
             )
-        cap_pick = tile("cap_pick", [P, PACK, O], F32)
-        for t in range(PACK):
-            nc.vector.tensor_copy(cap_pick[:, t, :], caps[:, t * V : (t + 1) * V].indirect(l4[:]))
-        capped = tile("capped", [P, PACK, O], F32)
-        nc.vector.tensor_tensor(capped[:], a_pick[:], cap_pick[:], ALU.min)
 
         b_rows = [tile("b_rows%d" % t, [P, J], F32) for t in range(PACK)]
         b_pick = tile("b_pick", [P, PACK, O], F32)
@@ -149,6 +145,14 @@ def tile_list_capped_twotab_further_plain_kernel(
             nc.vector.tensor_copy(b_rows[t][:], b_banks[t][:])
         for t in range(2, PACK):
             nc.vector.tensor_copy(b_pick[:, t, :], b_rows[t][:].indirect(l5[:]))
+
+        cap_pick = tile("cap_pick", [P, PACK, O], F32)
+        for t in range(2):
+            nc.scalar.activation(cap_pick[:, t, :], caps[:, t * V : (t + 1) * V].indirect(l4[:]), COPY)
+        for t in range(2, PACK):
+            nc.vector.tensor_copy(cap_pick[:, t, :], caps[:, t * V : (t + 1) * V].indirect(l4[:]))
+        capped = tile("capped", [P, PACK, O], F32)
+        nc.vector.tensor_tensor(capped[:], a_pick[:], cap_pick[:], ALU.min)
 
         hid = tile("hid", [P, O, PACK], BF16)
         nc.vector.tensor_tensor(

@@ -29,6 +29,16 @@ def load_scales(queue, plane, dram):
         queue.dma_start(out=plane[32 * q : 32 * q + 4, :].bitcast(I32), in_=dram[0, 4 * q : 4 * q + 4, :].bitcast(I32))
 
 
+def load_three(queue, plane, dram):
+    width = dram.shape[2] // 4
+    rows = dram[0, 0:14, :].bitcast(I32).unsqueeze(0).broadcast_to([5, 14, width])
+    queue.dma_start(out=plane[0:70, :].bitcast(I32), in_=rows)
+
+
+def load_last(queue, plane, dram):
+    queue.dma_start(out=plane[96:100, :].bitcast(I32), in_=dram[0, 12:16, :].bitcast(I32))
+
+
 def tile_list_capped_twotab_further_plain_kernel(
     tc, xt_words, xt_scales, w_words, w_scales, xo_words, xo_scales, w2_words, w2_scales, tb,
     wb_words, wb_scales, ws_words, ws_scales, offs, offs2, offs3, offs4, offs5, offs6, out,
@@ -55,7 +65,7 @@ def tile_list_capped_twotab_further_plain_kernel(
         w2_s = tile("w2_s", [P, R], U8)
         ws_s = tile("ws_s", [P, N], U8)
         wb_s = tile("wb_s", [P, N], U8)
-        for plane in (xt_s, w_s, xo_s, w2_s, ws_s, wb_s):
+        for plane in (xt_s, w_s, xo_s, w2_s,):
             nc.vector.memset(plane[:].bitcast(I32), 0)
 
         xt_w = tile("xt_w", [P, T], U16)
@@ -66,58 +76,67 @@ def tile_list_capped_twotab_further_plain_kernel(
         wb_w = tile("wb_w", [P, N], U32)
         caps = tile("caps", [P, PACK * V], F32)
 
-        load_words(nc.sync, w_w, merged(w_words))
-        l1 = load_list("l1", offs)
+        load_words(nc.gpsimd, xo_w, merged(xo_words))
+        nc.gpsimd.memset(ws_s[:].bitcast(I32), 0)
+        nc.gpsimd.memset(wb_s[:].bitcast(I32), 0)
+        nc.gpsimd.dma_start(out=caps[:, 0 : 2 * V], in_=tb.rearrange("(p t) v -> p (t v)", t=PACK)[:, 0 : 2 * V])
+        nc.gpsimd.dma_start(out=caps[:, 2 * V : 4 * V], in_=tb.rearrange("(p t) v -> p (t v)", t=PACK)[:, 2 * V : 4 * V])
+        load_words(nc.gpsimd, ws_w, merged(ws_words))
+        load_words(nc.gpsimd, wb_w, merged(wb_words))
         load_words(nc.sync, xt_w, xt_words[0])
+        l1 = load_list("l1", offs)
         load_scales(nc.sync, xt_s, xt_scales)
+        load_words(nc.sync, w_w, merged(w_words))
         l6 = load_list("l6", offs6)
         load_scales(nc.sync, w_s, w_scales)
+        load_words(nc.sync, w2_w, merged(w2_words))
         l2 = load_list("l2", offs2)
         load_scales(nc.sync, xo_s, xo_scales)
         l3 = load_list("l3", offs3)
         load_scales(nc.sync, w2_s, w2_scales)
-        l5 = load_list("l5", offs5)
         l4 = load_list("l4", offs4)
+        l5 = load_list("l5", offs5)
         load_scales(nc.sync, ws_s, ws_scales)
         load_scales(nc.sync, wb_s, wb_scales)
-        load_words(nc.gpsimd, xo_w, merged(xo_words))
-        load_words(nc.gpsimd, w2_w, merged(w2_words))
-        nc.gpsimd.dma_start(out=caps[:], in_=tb.rearrange("(p t) v -> p (t v)", t=PACK))
-        load_words(nc.gpsimd, ws_w, merged(ws_words))
-        load_words(nc.gpsimd, wb_w, merged(wb_words))
 
         def gather(name, window, lst, width, dtype):
             got = tile(name, [P, width], dtype)
             nc.vector.tensor_copy(got[:], window[:].indirect(lst[:]))
             return got
 
-        def deal(name, words, plane):
+        def move(engine, dst, src):
+            if engine == "V":
+                nc.vector.tensor_copy(dst, src)
+            else:
+                nc.scalar.activation(dst, src, COPY)
+
+        def deal(name, words, plane, engine):
             dw = tile(name + "_w", [P, PACK, P], U32)
             ds = tile(name + "_s", [P, PACK, P], U8)
-            nc.scalar.copy(dw[:].rearrange("p t q -> p q t"), words[:].rearrange("p (q t) -> p q t", t=PACK))
-            nc.vector.tensor_copy(ds[:].rearrange("p t q -> p q t"), plane[:].rearrange("p (q t) -> p q t", t=PACK))
+            copy = nc.vector.tensor_copy if engine == "V" else nc.scalar.copy
+            copy(dw[:].rearrange("p t (c i) -> p c t i", i=4), words[:].rearrange("p (c i t) -> p c t i", i=4, t=PACK))
+            nc.vector.tensor_copy(ds[:], plane[:].rearrange("p (q t) -> p t q", t=PACK))
             return dw, ds
 
         xg_w = gather("xg_w", xt_w, l1, J, U16)
         xg_s = gather("xg_s", xt_s, l1, J, U8)
-        wd_w, wd_s = deal("wd", w_w, w_s)
+        wd_w, wd_s = deal("wd", w_w, w_s, "A")
         a_pick = tile("a_pick", [P, PACK, O], F32)
-        a_banks = [ps.tile([P, 2, J], F32, name="a_bank%d" % h) for h in range(2)]
+        a_banks = [ps.tile([P, J], F32, name="a_bank%d" % t, tag="bank%d" % t) for t in range(PACK)]
         for t in range(PACK):
             nc.tensor.matmul_mx(
-                out=a_banks[t // 2][:, t % 2, :], lhsT=wd_w[:, t, :].bitcast(E5M2), lhsT_scale=wd_s[:, t, :],
+                out=a_banks[t][:], lhsT=wd_w[:, t, :].bitcast(E5M2), lhsT_scale=wd_s[:, t, :],
                 rhs=xg_w[:].bitcast(E2M1), rhs_scale=xg_s[:], start=True, stop=True,
             )
         a_rows = [tile("a_rows%d" % t, [P, J], F32) for t in range(PACK)]
-        for t in range(2):
-            nc.scalar.activation(a_rows[t][:], a_banks[0][:, t, :], COPY)
-            nc.vector.tensor_copy(a_rows[2 + t][:], a_banks[1][:, t, :])
         for t in range(PACK):
-            nc.scalar.activation(a_pick[:, t, :], a_rows[t][:].indirect(l3[:]), COPY)
+            move("AAAA"[t], a_rows[t][:], a_banks[t][:])
+        for t in range(PACK):
+            move("AAAA"[t], a_pick[:, t, :], a_rows[t][:].indirect(l3[:]))
 
         og_w = gather("og_w", xo_w, l2, J, U32)
         og_s = gather("og_s", xo_s, l2, J, U8)
-        w2d_w, w2d_s = deal("w2d", w2_w, w2_s)
+        w2d_w, w2d_s = deal("w2d", w2_w, w2_s, "A")
         b_banks = [ps.tile([P, J], F32, name="b_bank%d" % t) for t in range(PACK)]
         for t in range(PACK):
             nc.tensor.matmul_mx(
@@ -127,43 +146,40 @@ def tile_list_capped_twotab_further_plain_kernel(
 
         sg_w = gather("sg_w", xt_w, l6, O, U16)
         sg_s = gather("sg_s", xt_s, l6, O, U8)
-        y_banks = [ps.tile([P, O], F32, name="y_bank%d" % h) for h in range(2)]
+        y_banks = [ps.tile([P, O], F32, name="y_bank%d" % h, tag="bank%d" % h) for h in range(2)]
         for h in range(2):
             cols = slice(h * P, (h + 1) * P)
             nc.tensor.matmul_mx(
                 out=y_banks[h][:], lhsT=ws_w[:, cols].bitcast(E4M3), lhsT_scale=ws_s[:, cols],
                 rhs=sg_w[:].bitcast(E2M1), rhs_scale=sg_s[:], start=True, stop=False,
             )
-
+        cap_pick = tile("cap_pick", [P, PACK, O], F32)
+        for t in range(PACK):
+            move("VVVA"[t], cap_pick[:, t, :], caps[:, t * V : (t + 1) * V].indirect(l4[:]))
         b_rows = [tile("b_rows%d" % t, [P, J], F32) for t in range(PACK)]
         b_pick = tile("b_pick", [P, PACK, O], F32)
-        for t in range(2):
-            nc.scalar.activation(b_rows[t][:], b_banks[t][:], COPY)
-        for t in range(2):
-            nc.scalar.activation(b_pick[:, t, :], b_rows[t][:].indirect(l5[:]), COPY)
-        for t in range(2, PACK):
-            nc.vector.tensor_copy(b_rows[t][:], b_banks[t][:])
-        for t in range(2, PACK):
-            nc.vector.tensor_copy(b_pick[:, t, :], b_rows[t][:].indirect(l5[:]))
-
-        cap_pick = tile("cap_pick", [P, PACK, O], F32)
-        for t in range(2):
-            nc.scalar.activation(cap_pick[:, t, :], caps[:, t * V : (t + 1) * V].indirect(l4[:]), COPY)
-        for t in range(2, PACK):
-            nc.vector.tensor_copy(cap_pick[:, t, :], caps[:, t * V : (t + 1) * V].indirect(l4[:]))
+        for t in range(PACK):
+            move("VVAA"[t], b_rows[t][:], b_banks[t][:])
+        for t in range(PACK):
+            move("VVAA"[t], b_pick[:, t, :], b_rows[t][:].indirect(l5[:]))
         capped = tile("capped", [P, PACK, O], F32)
         nc.vector.tensor_tensor(capped[:], a_pick[:], cap_pick[:], ALU.min)
 
         hid = tile("hid", [P, O, PACK], BF16)
-        nc.vector.tensor_tensor(
-            hid[:].rearrange("p (c i) t -> p c t i", i=4),
-            capped[:].rearrange("p t (c i) -> p c t i", i=4),
-            b_pick[:].rearrange("p t (c i) -> p c t i", i=4),
-            ALU.max,
-        )
         hid_w = tile("hid_w", [P, O], U32)
         hid_s = tile("hid_s", [P, O], U8)
-        nc.vector.quantize_mx(out=hid_w[:].bitcast(E5M2), scales=hid_s[:], in_=hid[:].rearrange("p o t -> p (o t)"))
+        halves = [slice(0, O // 2), slice(O // 2, O)]
+        for half in halves:
+            nc.vector.tensor_tensor(
+                hid[:, half, :],
+                capped[:, :, half].rearrange("p t o -> p o t"),
+                b_pick[:, :, half].rearrange("p t o -> p o t"),
+                ALU.max,
+            )
+        for half in halves:
+            nc.vector.quantize_mx(
+                out=hid_w[:, half].bitcast(E5M2), scales=hid_s[:, half], in_=hid[:, half, :].rearrange("p o t -> p (o t)")
+            )
 
         for h in range(2):
             cols = slice(h * P, (h + 1) * P)

@@ -16,27 +16,27 @@ ALU = mybir.AluOpType
 
 P = 128
 PACK = 4
+QUADRANT = 32
+LINE = 4
+K_PASS = P * PACK
 T, Z, J, R, V, O, N = 1024, 1024, 256, 512, 512, 128, 256
-FLOPS = 2 * 512 * (R * J + R * J + N * O + N * O)
+FLOPS = 2 * K_PASS * (R * J + R * J + N * O + N * O)
+
+CAP_GATHERS_ON_VECTOR = 3
 
 
 def load_words(queue, tile, dram):
     queue.dma_start(out=tile[:].bitcast(I32), in_=dram.bitcast(I32))
 
 
-def load_scales(queue, plane, dram):
-    for q in range(4):
-        queue.dma_start(out=plane[32 * q : 32 * q + 4, :].bitcast(I32), in_=dram[0, 4 * q : 4 * q + 4, :].bitcast(I32))
+def load_plane(queue, plane, dram):
+    for q in range(P // QUADRANT):
+        rows = dram[0, 4 * q : 4 * q + 4, :]
+        queue.dma_start(out=plane[QUADRANT * q : QUADRANT * q + 4, :].bitcast(I32), in_=rows.bitcast(I32))
 
 
-def load_three(queue, plane, dram):
-    width = dram.shape[2] // 4
-    rows = dram[0, 0:14, :].bitcast(I32).unsqueeze(0).broadcast_to([5, 14, width])
-    queue.dma_start(out=plane[0:70, :].bitcast(I32), in_=rows)
-
-
-def load_last(queue, plane, dram):
-    queue.dma_start(out=plane[96:100, :].bitcast(I32), in_=dram[0, 12:16, :].bitcast(I32))
+def word_bytes(words):
+    return words[0].rearrange("p n t -> p (n t)")
 
 
 def tile_list_capped_twotab_further_plain_kernel(
@@ -45,151 +45,154 @@ def tile_list_capped_twotab_further_plain_kernel(
 ):
     nc = tc.nc
     with ExitStack() as ctx:
-        sb = ctx.enter_context(tc.tile_pool(name="sb", bufs=1))
-        ps = ctx.enter_context(tc.psum_pool(name="ps", bufs=1))
+        sbuf = ctx.enter_context(tc.tile_pool(name="sbuf", bufs=1))
+        psum = ctx.enter_context(tc.psum_pool(name="psum", bufs=1))
 
         def tile(name, shape, dtype):
-            return sb.tile(shape, dtype, name=name, align_bytes=64)
+            return sbuf.tile(shape, dtype, name=name, align_bytes=64)
 
         def load_list(name, dram):
-            lst = tile(name, [P, dram.shape[1]], U16)
-            nc.sync.dma_start(lst[:], dram)
-            return lst
+            offsets = tile(name, [P, dram.shape[1]], U16)
+            nc.sync.dma_start(offsets[:], dram)
+            return offsets
 
-        def merged(words):
-            return words[0].rearrange("p n t -> p (n t)")
+        def gather_packed(name, table, offsets, width, dtype):
+            picked = tile(name, [P, width], dtype)
+            nc.vector.tensor_copy(picked[:], table[:].indirect(offsets[:]))
+            return picked
 
-        xt_s = tile("xt_s", [P, T], U8)
-        w_s = tile("w_s", [P, R], U8)
-        xo_s = tile("xo_s", [P, Z], U8)
-        w2_s = tile("w2_s", [P, R], U8)
-        ws_s = tile("ws_s", [P, N], U8)
-        wb_s = tile("wb_s", [P, N], U8)
-        for plane in (xt_s, w_s, xo_s, w2_s,):
-            nc.vector.memset(plane[:].bitcast(I32), 0)
-
-        xt_w = tile("xt_w", [P, T], U16)
-        w_w = tile("w_w", [P, R], U32)
-        xo_w = tile("xo_w", [P, Z], U32)
-        w2_w = tile("w2_w", [P, R], U32)
-        ws_w = tile("ws_w", [P, N], U32)
-        wb_w = tile("wb_w", [P, N], U32)
-        caps = tile("caps", [P, PACK * V], F32)
-
-        load_words(nc.gpsimd, xo_w, merged(xo_words))
-        nc.gpsimd.memset(ws_s[:].bitcast(I32), 0)
-        nc.gpsimd.memset(wb_s[:].bitcast(I32), 0)
-        nc.gpsimd.dma_start(out=caps[:, 0 : 2 * V], in_=tb.rearrange("(p t) v -> p (t v)", t=PACK)[:, 0 : 2 * V])
-        nc.gpsimd.dma_start(out=caps[:, 2 * V : 4 * V], in_=tb.rearrange("(p t) v -> p (t v)", t=PACK)[:, 2 * V : 4 * V])
-        load_words(nc.gpsimd, ws_w, merged(ws_words))
-        load_words(nc.gpsimd, wb_w, merged(wb_words))
-        load_words(nc.sync, xt_w, xt_words[0])
-        l1 = load_list("l1", offs)
-        load_scales(nc.sync, xt_s, xt_scales)
-        load_words(nc.sync, w_w, merged(w_words))
-        l6 = load_list("l6", offs6)
-        load_scales(nc.sync, w_s, w_scales)
-        load_words(nc.sync, w2_w, merged(w2_words))
-        l2 = load_list("l2", offs2)
-        load_scales(nc.sync, xo_s, xo_scales)
-        l3 = load_list("l3", offs3)
-        load_scales(nc.sync, w2_s, w2_scales)
-        l4 = load_list("l4", offs4)
-        l5 = load_list("l5", offs5)
-        load_scales(nc.sync, ws_s, ws_scales)
-        load_scales(nc.sync, wb_s, wb_scales)
-
-        def gather(name, window, lst, width, dtype):
-            got = tile(name, [P, width], dtype)
-            nc.vector.tensor_copy(got[:], window[:].indirect(lst[:]))
-            return got
-
-        def move(engine, dst, src):
-            if engine == "V":
+        def copy_f32(on_vector, dst, src):
+            if on_vector:
                 nc.vector.tensor_copy(dst, src)
             else:
                 nc.scalar.activation(dst, src, COPY)
 
-        def deal(name, words, plane, engine):
-            dw = tile(name + "_w", [P, PACK, P], U32)
-            ds = tile(name + "_s", [P, PACK, P], U8)
-            copy = nc.vector.tensor_copy if engine == "V" else nc.scalar.copy
-            copy(dw[:].rearrange("p t (c i) -> p c t i", i=4), words[:].rearrange("p (c i t) -> p c t i", i=4, t=PACK))
-            nc.vector.tensor_copy(ds[:], plane[:].rearrange("p (q t) -> p t q", t=PACK))
-            return dw, ds
+        def regroup(name, words, plane):
+            words_tq = tile(name + "_words_tq", [P, PACK, P], U32)
+            plane_tq = tile(name + "_plane_tq", [P, PACK, P], U8)
+            nc.scalar.copy(
+                words_tq[:].rearrange("p t (c i) -> p c t i", i=LINE),
+                words[:].rearrange("p (c i t) -> p c t i", i=LINE, t=PACK),
+            )
+            nc.vector.tensor_copy(plane_tq[:], plane[:].rearrange("p (q t) -> p t q", t=PACK))
+            return words_tq, plane_tq
 
-        xg_w = gather("xg_w", xt_w, l1, J, U16)
-        xg_s = gather("xg_s", xt_s, l1, J, U8)
-        wd_w, wd_s = deal("wd", w_w, w_s, "A")
-        a_pick = tile("a_pick", [P, PACK, O], F32)
-        a_banks = [ps.tile([P, J], F32, name="a_bank%d" % t, tag="bank%d" % t) for t in range(PACK)]
+        xt_plane = tile("xt_plane", [P, T], U8)
+        w_plane = tile("w_plane", [P, R], U8)
+        xo_plane = tile("xo_plane", [P, Z], U8)
+        w2_plane = tile("w2_plane", [P, R], U8)
+        ws_plane = tile("ws_plane", [P, N], U8)
+        wb_plane = tile("wb_plane", [P, N], U8)
+        for plane in (xt_plane, w_plane, xo_plane, w2_plane, ws_plane, wb_plane):
+            nc.vector.memset(plane[:].bitcast(I32), 0)
+
+        xt_codes = tile("xt_codes", [P, T], U16)
+        w_codes = tile("w_codes", [P, R], U32)
+        xo_codes = tile("xo_codes", [P, Z], U32)
+        w2_codes = tile("w2_codes", [P, R], U32)
+        ws_codes = tile("ws_codes", [P, N], U32)
+        wb_codes = tile("wb_codes", [P, N], U32)
+        caps = tile("caps", [P, PACK * V], F32)
+        tb_rows = tb.rearrange("(p t) v -> p (t v)", t=PACK)
+        caps_halves = [slice(0, 2 * V), slice(2 * V, PACK * V)]
+
+        load_words(nc.gpsimd, xo_codes, word_bytes(xo_words))
+        load_words(nc.gpsimd, w2_codes, word_bytes(w2_words))
+
+        load_words(nc.sync, w_codes, word_bytes(w_words))
+        idx = load_list("idx", offs)
+        load_words(nc.sync, xt_codes, xt_words[0])
+        load_plane(nc.sync, xt_plane, xt_scales)
+        idx6 = load_list("idx6", offs6)
+        load_plane(nc.sync, w_plane, w_scales)
+        idx2 = load_list("idx2", offs2)
+        load_plane(nc.sync, xo_plane, xo_scales)
+        nc.sync.dma_start(out=caps[:, caps_halves[0]], in_=tb_rows[:, caps_halves[0]])
+        idx3 = load_list("idx3", offs3)
+        load_plane(nc.sync, w2_plane, w2_scales)
+        idx4 = load_list("idx4", offs4)
+        nc.sync.dma_start(out=caps[:, caps_halves[1]], in_=tb_rows[:, caps_halves[1]])
+        idx5 = load_list("idx5", offs5)
+        load_words(nc.sync, ws_codes, word_bytes(ws_words))
+        load_plane(nc.sync, ws_plane, ws_scales)
+        load_words(nc.sync, wb_codes, word_bytes(wb_words))
+        load_plane(nc.sync, wb_plane, wb_scales)
+
+        tokens_codes = gather_packed("tokens_codes", xt_codes, idx, J, U16)
+        tokens_plane = gather_packed("tokens_plane", xt_plane, idx, J, U8)
+        w_codes_tq, w_plane_tq = regroup("w", w_codes, w_plane)
+        a_picked = tile("a_picked", [P, PACK, O], F32)
+        a_banks = [psum.tile([P, J], F32, name="a_bank%d" % t, tag="a_bank%d" % t) for t in range(PACK)]
         for t in range(PACK):
             nc.tensor.matmul_mx(
-                out=a_banks[t][:], lhsT=wd_w[:, t, :].bitcast(E5M2), lhsT_scale=wd_s[:, t, :],
-                rhs=xg_w[:].bitcast(E2M1), rhs_scale=xg_s[:], start=True, stop=True,
+                out=a_banks[t][:], lhsT=w_codes_tq[:, t, :].bitcast(E5M2), lhsT_scale=w_plane_tq[:, t, :],
+                rhs=tokens_codes[:].bitcast(E2M1), rhs_scale=tokens_plane[:], start=True, stop=True,
             )
         a_rows = [tile("a_rows%d" % t, [P, J], F32) for t in range(PACK)]
         for t in range(PACK):
-            move("AAAA"[t], a_rows[t][:], a_banks[t][:])
+            nc.scalar.activation(a_rows[t][:], a_banks[t][:], COPY)
         for t in range(PACK):
-            move("AAAA"[t], a_pick[:, t, :], a_rows[t][:].indirect(l3[:]))
+            nc.scalar.activation(a_picked[:, t, :], a_rows[t][:].indirect(idx3[:]), COPY)
 
-        og_w = gather("og_w", xo_w, l2, J, U32)
-        og_s = gather("og_s", xo_s, l2, J, U8)
-        w2d_w, w2d_s = deal("w2d", w2_w, w2_s, "A")
-        b_banks = [ps.tile([P, J], F32, name="b_bank%d" % t) for t in range(PACK)]
+        notes_codes = gather_packed("notes_codes", xo_codes, idx2, J, U32)
+        notes_plane = gather_packed("notes_plane", xo_plane, idx2, J, U8)
+        w2_codes_tq, w2_plane_tq = regroup("w2", w2_codes, w2_plane)
+        b_banks = [psum.tile([P, J], F32, name="b_bank%d" % t) for t in range(PACK)]
         for t in range(PACK):
             nc.tensor.matmul_mx(
-                out=b_banks[t][:], lhsT=w2d_w[:, t, :].bitcast(E4M3), lhsT_scale=w2d_s[:, t, :],
-                rhs=og_w[:].bitcast(E5M2), rhs_scale=og_s[:], start=True, stop=True,
+                out=b_banks[t][:], lhsT=w2_codes_tq[:, t, :].bitcast(E4M3), lhsT_scale=w2_plane_tq[:, t, :],
+                rhs=notes_codes[:].bitcast(E5M2), rhs_scale=notes_plane[:], start=True, stop=True,
             )
 
-        sg_w = gather("sg_w", xt_w, l6, O, U16)
-        sg_s = gather("sg_s", xt_s, l6, O, U8)
-        y_banks = [ps.tile([P, O], F32, name="y_bank%d" % h, tag="bank%d" % h) for h in range(2)]
-        for h in range(2):
-            cols = slice(h * P, (h + 1) * P)
+        short_codes = gather_packed("short_codes", xt_codes, idx6, O, U16)
+        short_plane = gather_packed("short_plane", xt_plane, idx6, O, U8)
+        out_rows = [slice(h * P, (h + 1) * P) for h in range(N // P)]
+        out_banks = [psum.tile([P, O], F32, name="out_bank%d" % h, tag="a_bank%d" % h) for h in range(N // P)]
+        for bank, rows in zip(out_banks, out_rows):
             nc.tensor.matmul_mx(
-                out=y_banks[h][:], lhsT=ws_w[:, cols].bitcast(E4M3), lhsT_scale=ws_s[:, cols],
-                rhs=sg_w[:].bitcast(E2M1), rhs_scale=sg_s[:], start=True, stop=False,
+                out=bank[:], lhsT=ws_codes[:, rows].bitcast(E4M3), lhsT_scale=ws_plane[:, rows],
+                rhs=short_codes[:].bitcast(E2M1), rhs_scale=short_plane[:], start=True, stop=False,
             )
-        cap_pick = tile("cap_pick", [P, PACK, O], F32)
+
+        caps_picked = tile("caps_picked", [P, PACK, O], F32)
         for t in range(PACK):
-            move("VVVA"[t], cap_pick[:, t, :], caps[:, t * V : (t + 1) * V].indirect(l4[:]))
+            copy_f32(t < CAP_GATHERS_ON_VECTOR, caps_picked[:, t, :], caps[:, t * V : (t + 1) * V].indirect(idx4[:]))
         b_rows = [tile("b_rows%d" % t, [P, J], F32) for t in range(PACK)]
-        b_pick = tile("b_pick", [P, PACK, O], F32)
+        b_picked = tile("b_picked", [P, PACK, O], F32)
         for t in range(PACK):
-            move("VVAA"[t], b_rows[t][:], b_banks[t][:])
+            copy_f32(t % 2 == 0, b_rows[t][:], b_banks[t][:])
         for t in range(PACK):
-            move("VVAA"[t], b_pick[:, t, :], b_rows[t][:].indirect(l5[:]))
+            copy_f32(t % 2 == 0, b_picked[:, t, :], b_rows[t][:].indirect(idx5[:]))
+
         capped = tile("capped", [P, PACK, O], F32)
-        nc.vector.tensor_tensor(capped[:], a_pick[:], cap_pick[:], ALU.min)
+        for groups in (slice(0, 2), slice(2, PACK)):
+            nc.vector.tensor_tensor(capped[:, groups, :], a_picked[:, groups, :], caps_picked[:, groups, :], ALU.min)
 
         hid = tile("hid", [P, O, PACK], BF16)
-        hid_w = tile("hid_w", [P, O], U32)
-        hid_s = tile("hid_s", [P, O], U8)
-        halves = [slice(0, O // 2), slice(O // 2, O)]
-        for half in halves:
+        hid_codes = tile("hid_codes", [P, O], U32)
+        hid_plane = tile("hid_plane", [P, O], U8)
+        place_halves = [slice(0, O // 2), slice(O // 2, O)]
+        for places in place_halves:
             nc.vector.tensor_tensor(
-                hid[:, half, :],
-                capped[:, :, half].rearrange("p t o -> p o t"),
-                b_pick[:, :, half].rearrange("p t o -> p o t"),
+                hid[:, places, :],
+                capped[:, :, places].rearrange("p t o -> p o t"),
+                b_picked[:, :, places].rearrange("p t o -> p o t"),
                 ALU.max,
             )
-        for half in halves:
+        for places in place_halves:
             nc.vector.quantize_mx(
-                out=hid_w[:, half].bitcast(E5M2), scales=hid_s[:, half], in_=hid[:, half, :].rearrange("p o t -> p (o t)")
+                out=hid_codes[:, places].bitcast(E5M2), scales=hid_plane[:, places],
+                in_=hid[:, places, :].rearrange("p o t -> p (o t)"),
             )
 
-        for h in range(2):
-            cols = slice(h * P, (h + 1) * P)
+        for bank, rows in zip(out_banks, out_rows):
             nc.tensor.matmul_mx(
-                out=y_banks[h][:], lhsT=wb_w[:, cols].bitcast(E4M3), lhsT_scale=wb_s[:, cols],
-                rhs=hid_w[:].bitcast(E5M2), rhs_scale=hid_s[:], start=False, stop=True,
+                out=bank[:], lhsT=wb_codes[:, rows].bitcast(E4M3), lhsT_scale=wb_plane[:, rows],
+                rhs=hid_codes[:].bitcast(E5M2), rhs_scale=hid_plane[:], start=False, stop=True,
             )
-        y0 = tile("y0", [P, O], F32)
-        y1 = tile("y1", [P, O], F32)
-        nc.scalar.activation(y0[:], y_banks[0][:], COPY)
-        nc.scalar.dma_start(out=out[0:P, :], in_=y0[:])
-        nc.vector.tensor_copy(y1[:], y_banks[1][:])
-        nc.sync.dma_start(out=out[P : 2 * P, :], in_=y1[:])
+        out_upper = tile("out_upper", [P, O], F32)
+        out_lower = tile("out_lower", [P, O], F32)
+        nc.scalar.activation(out_upper[:], out_banks[0][:], COPY)
+        nc.scalar.dma_start(out=out[out_rows[0], :], in_=out_upper[:])
+        nc.vector.tensor_copy(out_lower[:], out_banks[1][:])
+        nc.sync.dma_start(out=out[out_rows[1], :], in_=out_lower[:])

from contextlib import ExitStack

import concourse.mybir as mybir

F32 = mybir.dt.float32
BF16 = mybir.dt.bfloat16
I32 = mybir.dt.int32
U32 = mybir.dt.uint32
U16 = mybir.dt.uint16
U8 = mybir.dt.uint8
E4M3 = mybir.dt.float8_e4m3fn_x4
E5M2 = mybir.dt.float8_e5m2_x4
E2M1 = mybir.dt.float4_e2m1fn_x4
COPY = mybir.ActivationFunctionType.Copy
ALU = mybir.AluOpType

P = 128
PACK = 4
QUADRANT = 32
LINE = 4
K_PASS = P * PACK
T, Z, J, R, V, O, N = 1024, 1024, 256, 512, 512, 128, 256
FLOPS = 2 * K_PASS * (R * J + R * J + N * O + N * O)

CAP_GATHERS_ON_VECTOR = 3


def load_words(queue, tile, dram):
    queue.dma_start(out=tile[:].bitcast(I32), in_=dram.bitcast(I32))


def load_plane(queue, plane, dram):
    for q in range(P // QUADRANT):
        rows = dram[0, 4 * q : 4 * q + 4, :]
        queue.dma_start(out=plane[QUADRANT * q : QUADRANT * q + 4, :].bitcast(I32), in_=rows.bitcast(I32))


def word_bytes(words):
    return words[0].rearrange("p n t -> p (n t)")


def tile_list_capped_twotab_further_plain_kernel(
    tc, xt_words, xt_scales, w_words, w_scales, xo_words, xo_scales, w2_words, w2_scales, tb,
    wb_words, wb_scales, ws_words, ws_scales, offs, offs2, offs3, offs4, offs5, offs6, out,
):
    nc = tc.nc
    with ExitStack() as ctx:
        sbuf = ctx.enter_context(tc.tile_pool(name="sbuf", bufs=1))
        psum = ctx.enter_context(tc.psum_pool(name="psum", bufs=1))

        def tile(name, shape, dtype):
            return sbuf.tile(shape, dtype, name=name, align_bytes=64)

        def load_list(name, dram):
            offsets = tile(name, [P, dram.shape[1]], U16)
            nc.sync.dma_start(offsets[:], dram)
            return offsets

        def gather_packed(name, table, offsets, width, dtype):
            picked = tile(name, [P, width], dtype)
            nc.vector.tensor_copy(picked[:], table[:].indirect(offsets[:]))
            return picked

        def copy_f32(on_vector, dst, src):
            if on_vector:
                nc.vector.tensor_copy(dst, src)
            else:
                nc.scalar.activation(dst, src, COPY)

        def regroup(name, words, plane):
            words_tq = tile(name + "_words_tq", [P, PACK, P], U32)
            plane_tq = tile(name + "_plane_tq", [P, PACK, P], U8)
            nc.scalar.copy(
                words_tq[:].rearrange("p t (c i) -> p c t i", i=LINE),
                words[:].rearrange("p (c i t) -> p c t i", i=LINE, t=PACK),
            )
            nc.vector.tensor_copy(plane_tq[:], plane[:].rearrange("p (q t) -> p t q", t=PACK))
            return words_tq, plane_tq

        xt_plane = tile("xt_plane", [P, T], U8)
        w_plane = tile("w_plane", [P, R], U8)
        xo_plane = tile("xo_plane", [P, Z], U8)
        w2_plane = tile("w2_plane", [P, R], U8)
        ws_plane = tile("ws_plane", [P, N], U8)
        wb_plane = tile("wb_plane", [P, N], U8)
        for plane in (xt_plane, w_plane, xo_plane, w2_plane, ws_plane, wb_plane):
            nc.vector.memset(plane[:].bitcast(I32), 0)

        xt_codes = tile("xt_codes", [P, T], U16)
        w_codes = tile("w_codes", [P, R], U32)
        xo_codes = tile("xo_codes", [P, Z], U32)
        w2_codes = tile("w2_codes", [P, R], U32)
        ws_codes = tile("ws_codes", [P, N], U32)
        wb_codes = tile("wb_codes", [P, N], U32)
        caps = tile("caps", [P, PACK * V], F32)
        tb_rows = tb.rearrange("(p t) v -> p (t v)", t=PACK)
        caps_halves = [slice(0, 2 * V), slice(2 * V, PACK * V)]

        load_words(nc.gpsimd, xo_codes, word_bytes(xo_words))
        load_words(nc.gpsimd, w2_codes, word_bytes(w2_words))

        load_words(nc.sync, w_codes, word_bytes(w_words))
        idx = load_list("idx", offs)
        load_words(nc.sync, xt_codes, xt_words[0])
        load_plane(nc.sync, xt_plane, xt_scales)
        idx6 = load_list("idx6", offs6)
        load_plane(nc.sync, w_plane, w_scales)
        idx2 = load_list("idx2", offs2)
        load_plane(nc.sync, xo_plane, xo_scales)
        nc.sync.dma_start(out=caps[:, caps_halves[0]], in_=tb_rows[:, caps_halves[0]])
        idx3 = load_list("idx3", offs3)
        load_plane(nc.sync, w2_plane, w2_scales)
        idx4 = load_list("idx4", offs4)
        nc.sync.dma_start(out=caps[:, caps_halves[1]], in_=tb_rows[:, caps_halves[1]])
        idx5 = load_list("idx5", offs5)
        load_words(nc.sync, ws_codes, word_bytes(ws_words))
        load_plane(nc.sync, ws_plane, ws_scales)
        load_words(nc.sync, wb_codes, word_bytes(wb_words))
        load_plane(nc.sync, wb_plane, wb_scales)

        tokens_codes = gather_packed("tokens_codes", xt_codes, idx, J, U16)
        tokens_plane = gather_packed("tokens_plane", xt_plane, idx, J, U8)
        w_codes_tq, w_plane_tq = regroup("w", w_codes, w_plane)
        a_picked = tile("a_picked", [P, PACK, O], F32)
        a_banks = [psum.tile([P, J], F32, name="a_bank%d" % t, tag="a_bank%d" % t) for t in range(PACK)]
        for t in range(PACK):
            nc.tensor.matmul_mx(
                out=a_banks[t][:], lhsT=w_codes_tq[:, t, :].bitcast(E5M2), lhsT_scale=w_plane_tq[:, t, :],
                rhs=tokens_codes[:].bitcast(E2M1), rhs_scale=tokens_plane[:], start=True, stop=True,
            )
        a_rows = [tile("a_rows%d" % t, [P, J], F32) for t in range(PACK)]
        for t in range(PACK):
            nc.scalar.activation(a_rows[t][:], a_banks[t][:], COPY)
        for t in range(PACK):
            nc.scalar.activation(a_picked[:, t, :], a_rows[t][:].indirect(idx3[:]), COPY)

        notes_codes = gather_packed("notes_codes", xo_codes, idx2, J, U32)
        notes_plane = gather_packed("notes_plane", xo_plane, idx2, J, U8)
        w2_codes_tq, w2_plane_tq = regroup("w2", w2_codes, w2_plane)
        b_banks = [psum.tile([P, J], F32, name="b_bank%d" % t) for t in range(PACK)]
        for t in range(PACK):
            nc.tensor.matmul_mx(
                out=b_banks[t][:], lhsT=w2_codes_tq[:, t, :].bitcast(E4M3), lhsT_scale=w2_plane_tq[:, t, :],
                rhs=notes_codes[:].bitcast(E5M2), rhs_scale=notes_plane[:], start=True, stop=True,
            )

        short_codes = gather_packed("short_codes", xt_codes, idx6, O, U16)
        short_plane = gather_packed("short_plane", xt_plane, idx6, O, U8)
        out_rows = [slice(h * P, (h + 1) * P) for h in range(N // P)]
        out_banks = [psum.tile([P, O], F32, name="out_bank%d" % h, tag="a_bank%d" % h) for h in range(N // P)]
        for bank, rows in zip(out_banks, out_rows):
            nc.tensor.matmul_mx(
                out=bank[:], lhsT=ws_codes[:, rows].bitcast(E4M3), lhsT_scale=ws_plane[:, rows],
                rhs=short_codes[:].bitcast(E2M1), rhs_scale=short_plane[:], start=True, stop=False,
            )

        caps_picked = tile("caps_picked", [P, PACK, O], F32)
        for t in range(PACK):
            copy_f32(t < CAP_GATHERS_ON_VECTOR, caps_picked[:, t, :], caps[:, t * V : (t + 1) * V].indirect(idx4[:]))
        b_rows = [tile("b_rows%d" % t, [P, J], F32) for t in range(PACK)]
        b_picked = tile("b_picked", [P, PACK, O], F32)
        for t in range(PACK):
            copy_f32(t % 2 == 0, b_rows[t][:], b_banks[t][:])
        for t in range(PACK):
            copy_f32(t % 2 == 0, b_picked[:, t, :], b_rows[t][:].indirect(idx5[:]))

        capped = tile("capped", [P, PACK, O], F32)
        for groups in (slice(0, 2), slice(2, PACK)):
            nc.vector.tensor_tensor(capped[:, groups, :], a_picked[:, groups, :], caps_picked[:, groups, :], ALU.min)

        hid = tile("hid", [P, O, PACK], BF16)
        hid_codes = tile("hid_codes", [P, O], U32)
        hid_plane = tile("hid_plane", [P, O], U8)
        place_halves = [slice(0, O // 2), slice(O // 2, O)]
        for places in place_halves:
            nc.vector.tensor_tensor(
                hid[:, places, :],
                capped[:, :, places].rearrange("p t o -> p o t"),
                b_picked[:, :, places].rearrange("p t o -> p o t"),
                ALU.max,
            )
        for places in place_halves:
            nc.vector.quantize_mx(
                out=hid_codes[:, places].bitcast(E5M2), scales=hid_plane[:, places],
                in_=hid[:, places, :].rearrange("p o t -> p (o t)"),
            )

        for bank, rows in zip(out_banks, out_rows):
            nc.tensor.matmul_mx(
                out=bank[:], lhsT=wb_codes[:, rows].bitcast(E4M3), lhsT_scale=wb_plane[:, rows],
                rhs=hid_codes[:].bitcast(E5M2), rhs_scale=hid_plane[:], start=False, stop=True,
            )
        out_upper = tile("out_upper", [P, O], F32)
        out_lower = tile("out_lower", [P, O], F32)
        nc.scalar.activation(out_upper[:], out_banks[0][:], COPY)
        nc.scalar.dma_start(out=out[out_rows[0], :], in_=out_upper[:])
        nc.vector.tensor_copy(out_lower[:], out_banks[1][:])
        nc.sync.dma_start(out=out[out_rows[1], :], in_=out_lower[:])
